import numpy as np
import ml_dtypes


def mxq(x, axis, fmt="e4m3"):
    dtype, down = {"e4m3": (ml_dtypes.float8_e4m3fn, 7), "e5m2": (ml_dtypes.float8_e5m2, 14)}[fmt]
    v = np.moveaxis(np.asarray(x, np.float32).astype(ml_dtypes.bfloat16).astype(np.float64), axis, -1)
    blocks = v.reshape(v.shape[:-1] + (-1, 32))
    amax = np.abs(blocks).max(-1, keepdims=True)
    byte = np.maximum(np.where(amax > 0, np.frexp(amax)[1] - 1 + 127, 0) - down, 1)
    scale = np.exp2(byte - 127.0)
    codes = (blocks / scale).astype(np.float32).astype(dtype).astype(np.float64)
    return np.moveaxis((codes * scale).reshape(v.shape), -1, axis)


WIDE = False


def mx_kscale(k):
    if not WIDE:
        return np.ones(k)
    levels = np.array([10, -10, 5, -5, 0])
    if k % 512:
        return np.exp2(np.random.permutation(np.resize(levels, k // 32))).repeat(32)
    a = np.empty((k // 512, 16))
    for p in range(k // 512):
        a[p, :8] = np.random.permutation(np.resize(levels, 8))
        for g in range(8):
            far = levels[np.abs(levels - a[p, g]) >= 10]
            a[p, g + 8] = far[np.random.randint(len(far))]
    return np.exp2(a.ravel()).repeat(32)


BF16 = ml_dtypes.bfloat16


def bf(x):
    return np.asarray(x, np.float32).astype(BF16)


def f64(x):
    return np.asarray(x).astype(np.float64)


E2M1 = np.array([0.0, 0.5, 1.0, 1.5, 2.0, 3.0, 4.0, 6.0, -0.0, -0.5, -1.0, -1.5, -2.0, -3.0, -4.0, -6.0])


def pack_weight(w, fmt):
    k, n = w.shape
    w = f64(bf(w)).reshape(k // 32, 32, n)
    amax = np.abs(w).max(1)
    if fmt == "e4m3":
        byte = np.frexp(amax)[1] - 1 + 127 - 7
    else:
        mant, ex = np.frexp(amax / 6.0)
        byte = np.where(mant > 0.5, ex, ex - 1) + 127
    byte = np.clip(np.where(amax > 0, byte, 1), 1, 254)
    scaled = (w * np.exp2(127.0 - byte)[:, None, :]).reshape(k, n).astype(np.float32)
    by_word = np.ascontiguousarray(scaled.reshape(k // 512, 128, 4, n).transpose(0, 1, 3, 2))
    if fmt == "e4m3":
        words = by_word.astype(ml_dtypes.float8_e4m3fn).view(np.uint8)
    else:
        c = by_word.astype(ml_dtypes.float4_e2m1fn).view(np.uint8) & 0xF
        words = c[..., 0::2] | (c[..., 1::2] << 4)
    return np.ascontiguousarray(words), np.ascontiguousarray(byte.astype(np.uint8).reshape(k // 512, 16, n))


def unpack_weight(words, scales, fmt):
    g, p, n, _ = words.shape
    if fmt == "e4m3":
        vals = np.ascontiguousarray(words).view(ml_dtypes.float8_e4m3fn).astype(np.float64)
    else:
        nib = np.empty((g, p, n, 4), np.uint8)
        nib[..., 0::2] = words & 0xF
        nib[..., 1::2] = words >> 4
        vals = E2M1[nib]
    vals = vals * np.repeat(np.exp2(scales.astype(np.float64) - 127.0), 8, axis=1)[..., None]
    return vals.transpose(0, 1, 3, 2).reshape(g * 512, n)
def pack4(w):
    words, scales = pack_weight(w, "e2m1")
    return words.reshape(words.shape[0], 128, -1), scales


def unpack4(words, scales):
    return unpack_weight(words.reshape(words.shape[0], 128, -1, 2), scales, "e2m1")


D, M, K, N, R = 4, 512, 1024, 1024, 512


def setup_inputs():
    s = mx_kscale(D * K)
    t = mx_kscale(D * N)
    strain = np.random.standard_normal((D, M, K)) * s.reshape(D, 1, K)
    gain = (1 + 0.1 * np.random.standard_normal((D, N))) * t.reshape(D, N)
    tmpl = np.random.standard_normal((D * K, N)) / np.sqrt(K) / s[:, None]
    cell = np.random.standard_normal((D * N, R)) / np.sqrt(D * N) / t[:, None]
    tmpl_words, tmpl_scales = pack4(tmpl)
    cell_words, cell_scales = pack4(cell)
    return {"strain": bf(strain), "gain": bf(gain),
            "tmpl_words": tmpl_words, "tmpl_scales": tmpl_scales,
            "cell_words": cell_words, "cell_scales": cell_scales}


def reference(strain, gain, tmpl_words, tmpl_scales, cell_words, cell_scales):
    tm = unpack4(tmpl_words, tmpl_scales).reshape(D, K, N)
    ce = unpack4(cell_words, cell_scales).reshape(D, N, R)
    z = mxq(f64(strain), 2, "e4m3") @ tm
    rho2 = z * z * f64(gain)[:, None, :]
    y = mxq(rho2, 2, "e4m3") @ ce
    return y.sum(axis=0)

@@ -1,0 +1,267 @@
+from contextlib import ExitStack
+
+import concourse.mybir as mybir
+from concourse.masks import make_identity
+
+D, M, K, N, R = 4, 512, 1024, 1024, 512
+FLOPS = 2 * D * M * K * N + 2 * D * M * N * R
+
+F32 = mybir.dt.float32
+BF16 = mybir.dt.bfloat16
+I32 = mybir.dt.int32
+U32 = mybir.dt.uint32
+U8 = mybir.dt.uint8
+FP8X4 = mybir.dt.float8_e4m3fn_x4
+FP4X4 = mybir.dt.float4_e2m1fn_x4
+ACT = mybir.ActivationFunctionType
+ALU = mybir.AluOpType
+
+P = 128
+BANK = 512
+PAIRS = M // (2 * P)
+STEPS = PAIRS * D
+ROT = 6
+
+
+def tile_detector_template_bank_s14_kernel(tc, strain, gain, tmpl_words, tmpl_scales, cell_words, cell_scales, out):
+    nc = tc.nc
+    with ExitStack() as ctx:
+        keep = ctx.enter_context(tc.tile_pool(name="keep", bufs=1))
+        work = ctx.enter_context(tc.tile_pool(name="work", bufs=2))
+        psum = ctx.enter_context(tc.psum_pool(name="psum", bufs=1))
+        ctx.enter_context(tc.manual_schedule())
+
+        uses = []
+
+        def next_bank(shape, dtype):
+            uses.append(len(uses))
+            return psum.tile(shape, dtype, name="rot%d" % (uses[-1] % ROT))
+
+        ident = keep.tile([P, P], F32, name="ident")
+        make_identity(nc, ident[:])
+        ident_bf = keep.tile([P, P], BF16, name="ident_bf")
+        make_identity(nc, ident_bf[:])
+
+        table_in = keep.tile([P, 8], F32, name="table_in")
+        table_out = keep.tile([P, 8], F32, name="table_out")
+        gain_rows = keep.tile([P, BANK], BF16, name="gain_rows")
+        nc.vector.memset(gain_rows[:], 0.0)
+        nc.vector.memset(table_in[:], 0.0)
+        nc.scalar.activation(out=table_out[:], in_=table_in[:], func=ACT.Square)
+
+        t_runs = [(0, 1), (1, 2), (2, 4)]
+        c_runs = [(0, 2), (2, 4)]
+        t_planes = []
+        for a, b in t_runs:
+            plane = keep.tile([P, 2 * (b - a), N], U8, name="tplane%d" % a, align_bytes=64)
+            t_planes.append(plane)
+        c_planes = []
+        for a, b in c_runs:
+            plane = keep.tile([P, 2 * (b - a), R], U8, name="cplane%d" % a, align_bytes=64)
+            c_planes.append(plane)
+        for plane in (t_planes[0], t_planes[1], c_planes[0], t_planes[2], c_planes[1]):
+            nc.vector.memset(plane[:].bitcast(I32), 0)
+
+        def load_plane(plane, scales, a, b):
+            rows = scales[2 * a : 2 * b].rearrange("g (q r) n -> r q g n", r=4)
+            for r in range(4):
+                nc.sync.dma_start(out=plane[r:P:32].bitcast(I32), in_=rows[r].bitcast(I32))
+
+        def t_scale(d, g, h):
+            for (a, b), plane in zip(t_runs, t_planes):
+                if a <= d < b:
+                    return plane[:, 2 * (d - a) + g, h * BANK : (h + 1) * BANK]
+
+        def c_scale(d, h):
+            for (a, b), plane in zip(c_runs, c_planes):
+                if a <= d < b:
+                    return plane[:, 2 * (d - a) + h, :]
+
+        x_tiles = {}
+        t_tiles = {}
+        c_tiles = {}
+
+        def load_x(s, i):
+            pair, d = divmod(s, D)
+            m0 = (2 * pair + i) * P
+            x = keep.tile([P, K], BF16, name="x%d_%d" % (s, i))
+            nc.sync.dma_start(out=x[:], in_=strain[d, m0 : m0 + P, :])
+            x_tiles[s, i] = x
+
+        def load_t(d, h0, h1):
+            w = keep.tile([P, 2, (h1 - h0) * 2 * BANK], U8, name="t%d_%d" % (d, h0), align_bytes=64)
+            src = tmpl_words[2 * d : 2 * d + 2].rearrange("g p n -> p g n")[:, :, h0 * 2 * BANK : h1 * 2 * BANK]
+            nc.sync.dma_start(out=w[:].bitcast(I32), in_=src.bitcast(I32))
+            for h in range(h0, h1):
+                for g in range(2):
+                    t_tiles[d, g, h] = w[:, g, (h - h0) * 2 * BANK : (h - h0 + 1) * 2 * BANK]
+
+        def load_c(d):
+            w = keep.tile([P, 2, 2 * R], U8, name="c%d" % d, align_bytes=64)
+            nc.sync.dma_start(out=w[:].bitcast(I32), in_=cell_words[2 * d : 2 * d + 2].rearrange("g p n -> p g n").bitcast(I32))
+            c_tiles[d] = w
+
+        load_x(0, 0)
+        load_t(0, 0, 1)
+        nc.sync.dma_start(out=gain_rows[0 : 2 * D, :], in_=gain.rearrange("d (h n) -> (d h) n", h=2))
+        load_plane(t_planes[0], tmpl_scales, 0, 1)
+        load_x(0, 1)
+        load_t(0, 1, 2)
+        load_x(1, 0)
+        load_x(1, 1)
+        load_t(1, 0, 2)
+        load_plane(t_planes[1], tmpl_scales, 1, 2)
+        load_plane(c_planes[0], cell_scales, 0, 2)
+        load_x(2, 0)
+        load_x(2, 1)
+        load_c(0)
+        load_x(3, 0)
+        load_x(3, 1)
+        load_plane(t_planes[2], tmpl_scales, 2, 4)
+        load_plane(c_planes[1], cell_scales, 2, 4)
+        load_t(2, 0, 2)
+        load_c(1)
+        load_x(4, 0)
+        load_x(4, 1)
+        load_t(3, 0, 2)
+        load_c(2)
+        load_x(5, 0)
+        load_x(5, 1)
+        load_c(3)
+        for s in range(6, STEPS):
+            load_x(s, 0)
+            load_x(s, 1)
+
+        gain_sorted = keep.tile([P, BANK], BF16, name="gain_sorted")
+        nc.vector.tensor_copy(
+            out=gain_sorted[:].rearrange("p (u q e) -> p u q e", u=2, e=2),
+            in_=gain_rows[:].rearrange("p (q u e) -> p u q e", u=2, e=2),
+        )
+        gains = {}
+
+        def spread_gain(d):
+            bank = next_bank([P, 2, BANK], BF16)
+            for h in range(2):
+                j = 2 * d + h
+                nc.tensor.matmul(bank[:, h, :], lhsT=ident_bf[:, j : j + 1].to_broadcast([P, P]), rhs=gain_sorted[:], start=True, stop=True)
+            gains[d] = keep.tile([P, 2, BANK], BF16, name="gain%d" % d)
+            return bank
+
+        def turn_strain(s, i):
+            words = x_tiles[s, i][:].bitcast(F32)
+            bank = next_bank([P, 4, P], F32)
+            for g in range(2):
+                for u in range(2):
+                    nc.tensor.transpose(bank[:, 2 * g + u, :], words[:, 2 * P * g + u : 2 * P * (g + 1) : 2], ident[:])
+            return bank
+
+        def turn_rho(halves):
+            bank = next_bank([P, 4, P], F32)
+            for h in range(2):
+                words = halves[h][:].bitcast(F32)
+                for u in range(2):
+                    nc.tensor.transpose(bank[:, 2 * h + u, :], words[:, u * P : (u + 1) * P], ident[:])
+            return bank
+
+        def gather_words(copy, grouped, i, bank):
+            dst = grouped[:].bitcast(F32)[:, i * BANK : (i + 1) * BANK]
+            copy(out=dst.rearrange("p (g m u) -> p g m u", g=2, u=2), in_=bank[:].rearrange("p (g u) m -> p g m u", u=2))
+
+        def quantise(grouped, codes, scales, i0, i1):
+            nc.vector.quantize_mx(
+                out=codes[:, i0 * 2 * P : i1 * 2 * P].bitcast(FP8X4),
+                scales=scales[:, i0 * 2 * P : i1 * 2 * P],
+                in_=grouped[:, i0 * 2 * BANK : i1 * 2 * BANK],
+            )
+
+        def new_operand(name, bufs):
+            grouped = work.tile([P, 4 * BANK], BF16, name=name + "_grouped", align_bytes=64)
+            codes = work.tile([P, BANK], U32, name=name + "_codes", align_bytes=64, bufs=bufs)
+            scales = work.tile([P, BANK], U8, name=name + "_scales", align_bytes=64, bufs=bufs)
+            return grouped, codes, scales
+
+        def stage_one(s, i, h, codes, scales):
+            d = s % D
+            z = next_bank([P, BANK], F32)
+            for g in range(2):
+                cols = slice((2 * i + g) * P, (2 * i + g + 1) * P)
+                nc.tensor.matmul_mx(
+                    out=z[:],
+                    lhsT=codes[:, cols].bitcast(FP8X4),
+                    lhsT_scale=scales[:, cols],
+                    rhs=t_tiles[d, g, h].bitcast(FP4X4),
+                    rhs_scale=t_scale(d, g, h),
+                    start=(g == 0),
+                    stop=(g == 1),
+                )
+            squared = work.tile([P, BANK], F32, name="squared", bufs=4)
+            nc.scalar.activation(
+                out=squared[:].rearrange("p (u q e) -> p u q e", u=2, e=2),
+                in_=z[:].rearrange("p (q u e) -> p u q e", u=2, e=2),
+                func=ACT.Square,
+            )
+            rho = work.tile([P, BANK], BF16, name="rho", bufs=8)
+            nc.vector.tensor_tensor(out=rho[:], in0=squared[:], in1=gains[d][:, h, :], op=ALU.mult)
+            return rho
+
+        sums = {}
+
+        def stage_two(s, i, codes, scales):
+            pair, d = divmod(s, D)
+            if d == 0:
+                sums[i] = psum.tile([P, R], F32, name="sum%d" % i)
+            for h in range(2):
+                cols = slice((2 * i + h) * P, (2 * i + h + 1) * P)
+                nc.tensor.matmul_mx(
+                    out=sums[i][:],
+                    lhsT=codes[:, cols].bitcast(FP8X4),
+                    lhsT_scale=scales[:, cols],
+                    rhs=c_tiles[d][:, h, :].bitcast(FP4X4),
+                    rhs_scale=c_scale(d, h),
+                    start=(d == 0 and h == 0),
+                    stop=(d == D - 1 and h == 1),
+                )
+            if d == D - 1:
+                result = work.tile([P, R], F32, name="result")
+                nc.scalar.copy(out=result[:], in_=sums[i][:])
+                m0 = (2 * pair + i) * P
+                nc.sync.dma_start(out=out[m0 : m0 + P, :], in_=result[:])
+
+        x_grouped, x_codes, x_scales = new_operand("x", 2)
+        bank = turn_strain(0, 0)
+        gather_words(nc.scalar.copy, x_grouped, 0, bank)
+        quantise(x_grouped, x_codes, x_scales, 0, 1)
+        for d in range(2):
+            bank = spread_gain(d)
+            nc.scalar.copy(out=gains[d][:], in_=bank[:])
+        bank = turn_strain(0, 1)
+        gather_words(nc.vector.tensor_copy, x_grouped, 1, bank)
+        for d in range(2, D):
+            bank = spread_gain(d)
+            nc.scalar.copy(out=gains[d][:], in_=bank[:])
+        quantise(x_grouped, x_codes, x_scales, 1, 2)
+
+        rhos = None
+        for s in range(STEPS + 1):
+            now = (x_codes, x_scales)
+            if s + 1 < STEPS:
+                x_grouped, x_codes, x_scales = new_operand("x", 2)
+                for i in range(2):
+                    bank = turn_strain(s + 1, i)
+                    gather_words(nc.scalar.copy, x_grouped, i, bank)
+            if s > 0:
+                r_grouped, r_codes, r_scales = new_operand("r", 2)
+                for i in range(2):
+                    bank = turn_rho(rhos[i])
+                    gather_words(nc.scalar.copy if i == 0 else nc.vector.tensor_copy, r_grouped, i, bank)
+            if s + 1 < STEPS:
+                quantise(x_grouped, x_codes, x_scales, 0, 2)
+            if 0 < s < STEPS:
+                quantise(r_grouped, r_codes, r_scales, 0, 2)
+            if s < STEPS:
+                rhos = [[stage_one(s, i, h, now[0], now[1]) for h in range(2)] for i in range(2)]
+            if s > 0:
+                for i in range(2):
+                    if s == STEPS:
+                        quantise(r_grouped, r_codes, r_scales, i, i + 1)
+                    stage_two(s - 1, i, r_codes, r_scales)

@@ -18,9 +18,13 @@ ALU = mybir.AluOpType
 
 P = 128
 BANK = 512
-PAIRS = M // (2 * P)
-STEPS = PAIRS * D
+ORDER = [(0, 0), (0, 1), (1, 0), (2, 0), (3, 0), (1, 1), (2, 1), (3, 1)]
+STEPS = len(ORDER)
+HELD = 1
 ROT = 6
+GAIN_AT = {2: 2, 3: 3}
+SORTED = (3, 4, 5, 6, 7)
+WARM = 0
 
 
 def tile_detector_template_bank_s14_kernel(tc, strain, gain, tmpl_words, tmpl_scales, cell_words, cell_scales, out):
@@ -33,21 +37,15 @@ def tile_detector_template_bank_s14_kernel(tc, strain, gain, tmpl_words, tmpl_sc
 
         uses = []
 
-        def next_bank(shape, dtype):
+        def next_bank(shape):
             uses.append(len(uses))
-            return psum.tile(shape, dtype, name="rot%d" % (uses[-1] % ROT))
+            return psum.tile(shape, F32, name="rot%d" % (uses[-1] % ROT))
 
         ident = keep.tile([P, P], F32, name="ident")
         make_identity(nc, ident[:])
-        ident_bf = keep.tile([P, P], BF16, name="ident_bf")
-        make_identity(nc, ident_bf[:])
 
         table_in = keep.tile([P, 8], F32, name="table_in")
         table_out = keep.tile([P, 8], F32, name="table_out")
-        gain_rows = keep.tile([P, BANK], BF16, name="gain_rows")
-        nc.vector.memset(gain_rows[:], 0.0)
-        nc.vector.memset(table_in[:], 0.0)
-        nc.scalar.activation(out=table_out[:], in_=table_in[:], func=ACT.Square)
 
         t_runs = [(0, 1), (1, 2), (2, 4)]
         c_runs = [(0, 2), (2, 4)]
@@ -59,7 +57,10 @@ def tile_detector_template_bank_s14_kernel(tc, strain, gain, tmpl_words, tmpl_sc
         for a, b in c_runs:
             plane = keep.tile([P, 2 * (b - a), R], U8, name="cplane%d" % a, align_bytes=64)
             c_planes.append(plane)
-        for plane in (t_planes[0], t_planes[1], c_planes[0], t_planes[2], c_planes[1]):
+        nc.vector.memset(t_planes[0][:].bitcast(I32), 0)
+        nc.vector.memset(table_in[:], 0.0)
+        nc.scalar.activation(out=table_out[:], in_=table_in[:], func=ACT.Square)
+        for plane in (c_planes[0], t_planes[1], t_planes[2], c_planes[1]):
             nc.vector.memset(plane[:].bitcast(I32), 0)
 
         def load_plane(plane, scales, a, b):
@@ -82,81 +83,97 @@ def tile_detector_template_bank_s14_kernel(tc, strain, gain, tmpl_words, tmpl_sc
         c_tiles = {}
 
         def load_x(s, i):
-            pair, d = divmod(s, D)
+            d, pair = ORDER[s]
             m0 = (2 * pair + i) * P
             x = keep.tile([P, K], BF16, name="x%d_%d" % (s, i))
             nc.sync.dma_start(out=x[:], in_=strain[d, m0 : m0 + P, :])
             x_tiles[s, i] = x
 
-        def load_t(d, h0, h1):
-            w = keep.tile([P, 2, (h1 - h0) * 2 * BANK], U8, name="t%d_%d" % (d, h0), align_bytes=64)
-            src = tmpl_words[2 * d : 2 * d + 2].rearrange("g p n -> p g n")[:, :, h0 * 2 * BANK : h1 * 2 * BANK]
-            nc.sync.dma_start(out=w[:].bitcast(I32), in_=src.bitcast(I32))
-            for h in range(h0, h1):
-                for g in range(2):
-                    t_tiles[d, g, h] = w[:, g, (h - h0) * 2 * BANK : (h - h0 + 1) * 2 * BANK]
+        def load_t(d):
+            w = keep.tile([P, 2, 2 * N], U8, name="t%d" % d, align_bytes=64)
+            nc.sync.dma_start(out=w[:].bitcast(I32), in_=tmpl_words[2 * d : 2 * d + 2].rearrange("g p n -> p g n").bitcast(I32))
+            t_tiles[d] = w
 
         def load_c(d):
             w = keep.tile([P, 2, 2 * R], U8, name="c%d" % d, align_bytes=64)
             nc.sync.dma_start(out=w[:].bitcast(I32), in_=cell_words[2 * d : 2 * d + 2].rearrange("g p n -> p g n").bitcast(I32))
             c_tiles[d] = w
 
+        gain_cols = keep.tile([P, 2 * D * 4], BF16, name="gain_cols")
+
+        def load_gain():
+            nc.sync.dma_start(
+                out=gain_cols[:].rearrange("q (j t) -> q j t", t=4),
+                in_=gain.rearrange("d (h q t) -> q (d h) t", h=2, t=4),
+            )
+
         load_x(0, 0)
-        load_t(0, 0, 1)
-        nc.sync.dma_start(out=gain_rows[0 : 2 * D, :], in_=gain.rearrange("d (h n) -> (d h) n", h=2))
-        load_plane(t_planes[0], tmpl_scales, 0, 1)
+        load_gain()
         load_x(0, 1)
-        load_t(0, 1, 2)
+        load_t(0)
+        load_plane(t_planes[0], tmpl_scales, *t_runs[0])
         load_x(1, 0)
         load_x(1, 1)
-        load_t(1, 0, 2)
-        load_plane(t_planes[1], tmpl_scales, 1, 2)
-        load_plane(c_planes[0], cell_scales, 0, 2)
         load_x(2, 0)
         load_x(2, 1)
+        load_plane(c_planes[0], cell_scales, *c_runs[0])
+        load_plane(t_planes[1], tmpl_scales, *t_runs[1])
         load_c(0)
+        load_t(1)
         load_x(3, 0)
         load_x(3, 1)
-        load_plane(t_planes[2], tmpl_scales, 2, 4)
-        load_plane(c_planes[1], cell_scales, 2, 4)
-        load_t(2, 0, 2)
-        load_c(1)
         load_x(4, 0)
         load_x(4, 1)
-        load_t(3, 0, 2)
-        load_c(2)
+        load_plane(t_planes[2], tmpl_scales, *t_runs[2])
+        load_plane(c_planes[1], cell_scales, *c_runs[1])
+        load_t(2)
+        load_c(1)
         load_x(5, 0)
         load_x(5, 1)
+        load_t(3)
+        load_c(2)
+        load_x(6, 0)
+        load_x(6, 1)
         load_c(3)
-        for s in range(6, STEPS):
-            load_x(s, 0)
-            load_x(s, 1)
+        load_x(7, 0)
+        load_x(7, 1)
 
-        gain_sorted = keep.tile([P, BANK], BF16, name="gain_sorted")
-        nc.vector.tensor_copy(
-            out=gain_sorted[:].rearrange("p (u q e) -> p u q e", u=2, e=2),
-            in_=gain_rows[:].rearrange("p (q u e) -> p u q e", u=2, e=2),
-        )
         gains = {}
 
-        def spread_gain(d):
-            bank = next_bank([P, 2, BANK], BF16)
-            for h in range(2):
-                j = 2 * d + h
-                nc.tensor.matmul(bank[:, h, :], lhsT=ident_bf[:, j : j + 1].to_broadcast([P, P]), rhs=gain_sorted[:], start=True, stop=True)
-            gains[d] = keep.tile([P, 2, BANK], BF16, name="gain%d" % d)
-            return bank
+        def spread_gain(d, copy):
+            words = gain_cols[:].bitcast(F32)
+            bank = next_bank([P, 4, P])
+            for j in range(4):
+                nc.tensor.transpose(bank[:, j, :], words[:, 4 * d + j : 4 * d + j + 1].to_broadcast([P, P]), ident[:])
+            gains[d] = keep.tile([P, N], BF16, name="gain%d" % d)
+            if copy is None:
+                return bank
+            copy(out=gains[d][:].bitcast(F32), in_=bank[:].rearrange("p j q -> p (j q)"))
+
+        sorted_x = {}
+
+        def sort_strain(s):
+            for i in range(2):
+                tidy = work.tile([P, BANK], F32, name="tidy", bufs=4)
+                nc.vector.tensor_copy(
+                    out=tidy[:].rearrange("p (g u q) -> p g u q", g=2, u=2),
+                    in_=x_tiles[s, i][:].bitcast(F32).rearrange("p (g q u) -> p g u q", g=2, u=2),
+                )
+                sorted_x[s, i] = tidy
 
         def turn_strain(s, i):
-            words = x_tiles[s, i][:].bitcast(F32)
-            bank = next_bank([P, 4, P], F32)
+            bank = next_bank([P, 4, P])
             for g in range(2):
                 for u in range(2):
-                    nc.tensor.transpose(bank[:, 2 * g + u, :], words[:, 2 * P * g + u : 2 * P * (g + 1) : 2], ident[:])
+                    if s in SORTED:
+                        src = sorted_x[s, i][:, (2 * g + u) * P : (2 * g + u + 1) * P]
+                    else:
+                        src = x_tiles[s, i][:].bitcast(F32)[:, 2 * P * g + u : 2 * P * (g + 1) : 2]
+                    nc.tensor.transpose(bank[:, 2 * g + u, :], src, ident[:])
             return bank
 
         def turn_rho(halves):
-            bank = next_bank([P, 4, P], F32)
+            bank = next_bank([P, 4, P])
             for h in range(2):
                 words = halves[h][:].bitcast(F32)
                 for u in range(2):
@@ -174,22 +191,22 @@ def tile_detector_template_bank_s14_kernel(tc, strain, gain, tmpl_words, tmpl_sc
                 in_=grouped[:, i0 * 2 * BANK : i1 * 2 * BANK],
             )
 
-        def new_operand(name, bufs):
+        def new_operand(name, tag):
             grouped = work.tile([P, 4 * BANK], BF16, name=name + "_grouped", align_bytes=64)
-            codes = work.tile([P, BANK], U32, name=name + "_codes", align_bytes=64, bufs=bufs)
-            scales = work.tile([P, BANK], U8, name=name + "_scales", align_bytes=64, bufs=bufs)
+            codes = work.tile([P, BANK], U32, name=tag + "_codes", align_bytes=64)
+            scales = work.tile([P, BANK], U8, name=tag + "_scales", align_bytes=64)
             return grouped, codes, scales
 
         def stage_one(s, i, h, codes, scales):
-            d = s % D
-            z = next_bank([P, BANK], F32)
+            d = ORDER[s][0]
+            z = next_bank([P, BANK])
             for g in range(2):
                 cols = slice((2 * i + g) * P, (2 * i + g + 1) * P)
                 nc.tensor.matmul_mx(
                     out=z[:],
                     lhsT=codes[:, cols].bitcast(FP8X4),
                     lhsT_scale=scales[:, cols],
-                    rhs=t_tiles[d, g, h].bitcast(FP4X4),
+                    rhs=t_tiles[d][:, g, h * 2 * BANK : (h + 1) * 2 * BANK].bitcast(FP4X4),
                     rhs_scale=t_scale(d, g, h),
                     start=(g == 0),
                     stop=(g == 1),
@@ -201,14 +218,17 @@ def tile_detector_template_bank_s14_kernel(tc, strain, gain, tmpl_words, tmpl_sc
                 func=ACT.Square,
             )
             rho = work.tile([P, BANK], BF16, name="rho", bufs=8)
-            nc.vector.tensor_tensor(out=rho[:], in0=squared[:], in1=gains[d][:, h, :], op=ALU.mult)
+            nc.vector.tensor_tensor(out=rho[:], in0=squared[:], in1=gains[d][:, h * BANK : (h + 1) * BANK], op=ALU.mult)
             return rho
 
         sums = {}
+        added = {}
 
         def stage_two(s, i, codes, scales):
-            pair, d = divmod(s, D)
-            if d == 0:
+            d, pair = ORDER[s]
+            done = added.get((pair, i), 0)
+            added[pair, i] = done + 1
+            if done == 0:
                 sums[i] = psum.tile([P, R], F32, name="sum%d" % i)
             for h in range(2):
                 cols = slice((2 * i + h) * P, (2 * i + h + 1) * P)
@@ -218,50 +238,72 @@ def tile_detector_template_bank_s14_kernel(tc, strain, gain, tmpl_words, tmpl_sc
                     lhsT_scale=scales[:, cols],
                     rhs=c_tiles[d][:, h, :].bitcast(FP4X4),
                     rhs_scale=c_scale(d, h),
-                    start=(d == 0 and h == 0),
-                    stop=(d == D - 1 and h == 1),
+                    start=(done == 0 and h == 0),
+                    stop=(done == D - 1 and h == 1),
                 )
-            if d == D - 1:
-                result = work.tile([P, R], F32, name="result")
-                nc.scalar.copy(out=result[:], in_=sums[i][:])
+            if done == D - 1:
                 m0 = (2 * pair + i) * P
-                nc.sync.dma_start(out=out[m0 : m0 + P, :], in_=result[:])
+                if pair == 1 and i == 1:
+                    for c0 in (0, R // 2):
+                        half = work.tile([P, R // 2], F32, name="half")
+                        nc.scalar.copy(out=half[:], in_=sums[i][:, c0 : c0 + R // 2])
+                        nc.sync.dma_start(out=out[m0 : m0 + P, c0 : c0 + R // 2], in_=half[:])
+                else:
+                    result = work.tile([P, R], F32, name="result")
+                    (nc.vector.tensor_copy if pair == 1 else nc.scalar.copy)(out=result[:], in_=sums[i][:])
+                    nc.sync.dma_start(out=out[m0 : m0 + P, :], in_=result[:])
 
-        x_grouped, x_codes, x_scales = new_operand("x", 2)
+        x_grouped, x_codes, x_scales = new_operand("x", "x")
         bank = turn_strain(0, 0)
         gather_words(nc.scalar.copy, x_grouped, 0, bank)
         quantise(x_grouped, x_codes, x_scales, 0, 1)
-        for d in range(2):
-            bank = spread_gain(d)
-            nc.scalar.copy(out=gains[d][:], in_=bank[:])
         bank = turn_strain(0, 1)
-        gather_words(nc.vector.tensor_copy, x_grouped, 1, bank)
-        for d in range(2, D):
-            bank = spread_gain(d)
-            nc.scalar.copy(out=gains[d][:], in_=bank[:])
+        gather_words(nc.scalar.copy, x_grouped, 1, bank)
         quantise(x_grouped, x_codes, x_scales, 1, 2)
+        for d in range(2):
+            spread_gain(d, nc.vector.tensor_copy if d % 2 == 0 else nc.scalar.copy)
 
         rhos = None
+        held = None
         for s in range(STEPS + 1):
             now = (x_codes, x_scales)
+            if s + 2 in SORTED and s > 1:
+                sort_strain(s + 2)
+            if s == 0:
+                rhos = [[stage_one(s, i, h, now[0], now[1]) for h in range(2)] for i in range(1)]
             if s + 1 < STEPS:
-                x_grouped, x_codes, x_scales = new_operand("x", 2)
+                x_grouped, x_codes, x_scales = new_operand("x", "x")
                 for i in range(2):
                     bank = turn_strain(s + 1, i)
                     gather_words(nc.scalar.copy, x_grouped, i, bank)
+            if s in GAIN_AT:
+                late_gain = spread_gain(GAIN_AT[s], None)
             if s > 0:
-                r_grouped, r_codes, r_scales = new_operand("r", 2)
+                r_grouped, r_codes, r_scales = new_operand("r", "held" if s - 1 == HELD else "r")
                 for i in range(2):
                     bank = turn_rho(rhos[i])
                     gather_words(nc.scalar.copy if i == 0 else nc.vector.tensor_copy, r_grouped, i, bank)
+            if s in GAIN_AT:
+                nc.scalar.copy(out=gains[GAIN_AT[s]][:].bitcast(F32), in_=late_gain[:].rearrange("p j q -> p (j q)"))
             if s + 1 < STEPS:
                 quantise(x_grouped, x_codes, x_scales, 0, 2)
             if 0 < s < STEPS:
                 quantise(r_grouped, r_codes, r_scales, 0, 2)
-            if s < STEPS:
+            if s + 2 in SORTED and s <= 1:
+                sort_strain(s + 2)
+            if s == 0:
+                rhos.append([stage_one(s, 1, h, now[0], now[1]) for h in range(2)])
+            elif s < STEPS:
                 rhos = [[stage_one(s, i, h, now[0], now[1]) for h in range(2)] for i in range(2)]
-            if s > 0:
+            if s - 1 == HELD:
+                held = (r_codes, r_scales)
+            elif s == STEPS:
                 for i in range(2):
-                    if s == STEPS:
-                        quantise(r_grouped, r_codes, r_scales, i, i + 1)
+                    quantise(r_grouped, r_codes, r_scales, i, i + 1)
+                for i in range(2):
+                    stage_two(HELD, i, held[0], held[1])
+                for i in range(2):
+                    stage_two(s - 1, i, r_codes, r_scales)
+            elif s > 0:
+                for i in range(2):
                     stage_two(s - 1, i, r_codes, r_scales)

@@ -22,7 +22,7 @@ ORDER = [(0, 0), (0, 1), (1, 0), (2, 0), (3, 0), (1, 1), (2, 1), (3, 1)]
 STEPS = len(ORDER)
 HELD = 1
 ROT = 6
-GAIN_AT = {2: 2, 3: 3}
+GAIN_AT = {0: (0,), 1: (1,), 2: (2,), 3: (3,)}
 SORTED = (3, 4, 5, 6, 7)
 WARM = 0
 
@@ -57,6 +57,8 @@ def tile_detector_template_bank_s14_kernel(tc, strain, gain, tmpl_words, tmpl_sc
         for a, b in c_runs:
             plane = keep.tile([P, 2 * (b - a), R], U8, name="cplane%d" % a, align_bytes=64)
             c_planes.append(plane)
+        gain_rows = keep.tile([P, BANK], BF16, name="gain_rows")
+        nc.vector.memset(gain_rows[:], 0.0)
         nc.vector.memset(t_planes[0][:].bitcast(I32), 0)
         nc.vector.memset(table_in[:], 0.0)
         nc.scalar.activation(out=table_out[:], in_=table_in[:], func=ACT.Square)
@@ -79,15 +81,18 @@ def tile_detector_template_bank_s14_kernel(tc, strain, gain, tmpl_words, tmpl_sc
                     return plane[:, 2 * (d - a) + h, :]
 
         x_tiles = {}
+        x_whole = {}
         t_tiles = {}
         c_tiles = {}
 
-        def load_x(s, i):
+        def load_x(s, i0, i1):
             d, pair = ORDER[s]
-            m0 = (2 * pair + i) * P
-            x = keep.tile([P, K], BF16, name="x%d_%d" % (s, i))
-            nc.sync.dma_start(out=x[:], in_=strain[d, m0 : m0 + P, :])
-            x_tiles[s, i] = x
+            rows = strain[d, (2 * pair + i0) * P : (2 * pair + i1) * P, :]
+            x = keep.tile([P, i1 - i0, K], BF16, name="x%d_%d" % (s, i0))
+            nc.sync.dma_start(out=x[:], in_=rows.rearrange("(i m) k -> m i k", m=P))
+            x_whole[s] = x
+            for i in range(i0, i1):
+                x_tiles[s, i] = x[:, i - i0, :]
 
         def load_t(d):
             w = keep.tile([P, 2, 2 * N], U8, name="t%d" % d, align_bytes=64)
@@ -99,67 +104,66 @@ def tile_detector_template_bank_s14_kernel(tc, strain, gain, tmpl_words, tmpl_sc
             nc.sync.dma_start(out=w[:].bitcast(I32), in_=cell_words[2 * d : 2 * d + 2].rearrange("g p n -> p g n").bitcast(I32))
             c_tiles[d] = w
 
-        gain_cols = keep.tile([P, 2 * D * 4], BF16, name="gain_cols")
-
         def load_gain():
-            nc.sync.dma_start(
-                out=gain_cols[:].rearrange("q (j t) -> q j t", t=4),
-                in_=gain.rearrange("d (h q t) -> q (d h) t", h=2, t=4),
-            )
+            nc.sync.dma_start(out=gain_rows[0 : 2 * D, :], in_=gain.rearrange("d (h n) -> (d h) n", h=2))
 
-        load_x(0, 0)
-        load_gain()
-        load_x(0, 1)
+        load_x(0, 0, 1)
+        load_x(0, 1, 2)
         load_t(0)
+        load_gain()
         load_plane(t_planes[0], tmpl_scales, *t_runs[0])
-        load_x(1, 0)
-        load_x(1, 1)
-        load_x(2, 0)
-        load_x(2, 1)
-        load_plane(c_planes[0], cell_scales, *c_runs[0])
+        load_x(1, 0, 1)
+        load_x(1, 1, 2)
+        load_x(2, 0, 2)
+        load_x(3, 0, 2)
         load_plane(t_planes[1], tmpl_scales, *t_runs[1])
-        load_c(0)
         load_t(1)
-        load_x(3, 0)
-        load_x(3, 1)
-        load_x(4, 0)
-        load_x(4, 1)
+        load_x(4, 0, 2)
+        load_plane(c_planes[0], cell_scales, *c_runs[0])
+        load_c(0)
         load_plane(t_planes[2], tmpl_scales, *t_runs[2])
         load_plane(c_planes[1], cell_scales, *c_runs[1])
         load_t(2)
         load_c(1)
-        load_x(5, 0)
-        load_x(5, 1)
+        load_x(5, 0, 2)
         load_t(3)
         load_c(2)
-        load_x(6, 0)
-        load_x(6, 1)
+        load_x(6, 0, 2)
         load_c(3)
-        load_x(7, 0)
-        load_x(7, 1)
+        load_x(7, 0, 2)
 
         gains = {}
+        gain_cols = keep.tile([P, 4 * D], F32, name="gain_cols")
+
+        def turn_gain():
+            bank = next_bank([P, 2, P])
+            for u in range(2):
+                nc.tensor.transpose(bank[:, u, :], gain_rows[:].bitcast(F32)[:, u : 2 * P : 2], ident[:])
+            nc.vector.tensor_copy(
+                out=gain_cols[:].rearrange("p (j u) -> p j u", u=2),
+                in_=bank[:, :, 0 : 2 * D].rearrange("p u j -> p j u"),
+            )
 
         def spread_gain(d, copy):
-            words = gain_cols[:].bitcast(F32)
+            words = gain_cols[:]
             bank = next_bank([P, 4, P])
             for j in range(4):
                 nc.tensor.transpose(bank[:, j, :], words[:, 4 * d + j : 4 * d + j + 1].to_broadcast([P, P]), ident[:])
             gains[d] = keep.tile([P, N], BF16, name="gain%d" % d)
-            if copy is None:
-                return bank
             copy(out=gains[d][:].bitcast(F32), in_=bank[:].rearrange("p j q -> p (j q)"))
 
         sorted_x = {}
+        squares = {}
+        rhos = {}
 
         def sort_strain(s):
+            tidy = work.tile([P, 2 * BANK], F32, name="tidy")
+            nc.vector.tensor_copy(
+                out=tidy[:].rearrange("p (j u q) -> p j u q", j=4, u=2),
+                in_=x_whole[s][:].rearrange("p i k -> p (i k)").bitcast(F32).rearrange("p (j q u) -> p j u q", j=4, u=2),
+            )
             for i in range(2):
-                tidy = work.tile([P, BANK], F32, name="tidy", bufs=4)
-                nc.vector.tensor_copy(
-                    out=tidy[:].rearrange("p (g u q) -> p g u q", g=2, u=2),
-                    in_=x_tiles[s, i][:].bitcast(F32).rearrange("p (g q u) -> p g u q", g=2, u=2),
-                )
-                sorted_x[s, i] = tidy
+                sorted_x[s, i] = tidy[:, i * BANK : (i + 1) * BANK]
 
         def turn_strain(s, i):
             bank = next_bank([P, 4, P])
@@ -168,16 +172,15 @@ def tile_detector_template_bank_s14_kernel(tc, strain, gain, tmpl_words, tmpl_sc
                     if s in SORTED:
                         src = sorted_x[s, i][:, (2 * g + u) * P : (2 * g + u + 1) * P]
                     else:
-                        src = x_tiles[s, i][:].bitcast(F32)[:, 2 * P * g + u : 2 * P * (g + 1) : 2]
+                        src = x_tiles[s, i].bitcast(F32)[:, 2 * P * g + u : 2 * P * (g + 1) : 2]
                     nc.tensor.transpose(bank[:, 2 * g + u, :], src, ident[:])
             return bank
 
-        def turn_rho(halves):
+        def turn_rho(s, i):
+            words = rhos[s, i][:].bitcast(F32)
             bank = next_bank([P, 4, P])
-            for h in range(2):
-                words = halves[h][:].bitcast(F32)
-                for u in range(2):
-                    nc.tensor.transpose(bank[:, 2 * h + u, :], words[:, u * P : (u + 1) * P], ident[:])
+            for j in range(4):
+                nc.tensor.transpose(bank[:, j, :], words[:, j * P : (j + 1) * P], ident[:])
             return bank
 
         def gather_words(copy, grouped, i, bank):
@@ -211,15 +214,20 @@ def tile_detector_template_bank_s14_kernel(tc, strain, gain, tmpl_words, tmpl_sc
                     start=(g == 0),
                     stop=(g == 1),
                 )
-            squared = work.tile([P, BANK], F32, name="squared", bufs=4)
+            if h == 0:
+                squares[s, i] = work.tile([P, N], F32, name="squared", bufs=3)
             nc.scalar.activation(
-                out=squared[:].rearrange("p (u q e) -> p u q e", u=2, e=2),
+                out=squares[s, i][:, h * BANK : (h + 1) * BANK].rearrange("p (u q e) -> p u q e", u=2, e=2),
                 in_=z[:].rearrange("p (q u e) -> p u q e", u=2, e=2),
                 func=ACT.Square,
             )
-            rho = work.tile([P, BANK], BF16, name="rho", bufs=8)
-            nc.vector.tensor_tensor(out=rho[:], in0=squared[:], in1=gains[d][:, h * BANK : (h + 1) * BANK], op=ALU.mult)
-            return rho
+
+        def weigh(s, i, parts):
+            d = ORDER[s][0]
+            rhos[s, i] = work.tile([P, N], BF16, name="rho", bufs=6)
+            for c0 in range(0, N, N // parts):
+                cols = slice(c0, c0 + N // parts)
+                nc.vector.tensor_tensor(out=rhos[s, i][:, cols], in0=squares[s, i][:, cols], in1=gains[d][:, cols], op=ALU.mult)
 
         sums = {}
         added = {}
@@ -260,50 +268,63 @@ def tile_detector_template_bank_s14_kernel(tc, strain, gain, tmpl_words, tmpl_sc
         bank = turn_strain(0, 1)
         gather_words(nc.scalar.copy, x_grouped, 1, bank)
         quantise(x_grouped, x_codes, x_scales, 1, 2)
-        for d in range(2):
-            spread_gain(d, nc.vector.tensor_copy if d % 2 == 0 else nc.scalar.copy)
+        turn_gain()
 
-        rhos = None
-        held = None
-        for s in range(STEPS + 1):
-            now = (x_codes, x_scales)
-            if s + 2 in SORTED and s > 1:
-                sort_strain(s + 2)
+        x_ops = {0: (x_codes, x_scales)}
+        r_ops = {}
+        LAST = STEPS - 1
+
+        def rho_side(s, i):
+            if i == 0:
+                r_ops[s] = new_operand("r", "held" if s == HELD else "r")
+            bank = turn_rho(s, i)
+            gather_words(nc.scalar.copy if i == 0 or s in (6, 7) else nc.vector.tensor_copy, r_ops[s][0], i, bank)
+
+        for s in range(STEPS):
+            if s > 0:
+                weigh(s - 1, 1, 1)
             if s == 0:
-                rhos = [[stage_one(s, i, h, now[0], now[1]) for h in range(2)] for i in range(1)]
-            if s + 1 < STEPS:
+                for h in range(2):
+                    stage_one(s, 0, h, *x_ops[s])
+            if s >= 2:
+                for i in range(2):
+                    rho_side(s - 2, i)
+            if s < LAST:
                 x_grouped, x_codes, x_scales = new_operand("x", "x")
+                x_ops[s + 1] = (x_codes, x_scales)
                 for i in range(2):
                     bank = turn_strain(s + 1, i)
-                    gather_words(nc.scalar.copy, x_grouped, i, bank)
-            if s in GAIN_AT:
-                late_gain = spread_gain(GAIN_AT[s], None)
-            if s > 0:
-                r_grouped, r_codes, r_scales = new_operand("r", "held" if s - 1 == HELD else "r")
-                for i in range(2):
-                    bank = turn_rho(rhos[i])
-                    gather_words(nc.scalar.copy if i == 0 else nc.vector.tensor_copy, r_grouped, i, bank)
-            if s in GAIN_AT:
-                nc.scalar.copy(out=gains[GAIN_AT[s]][:].bitcast(F32), in_=late_gain[:].rearrange("p j q -> p (j q)"))
-            if s + 1 < STEPS:
-                quantise(x_grouped, x_codes, x_scales, 0, 2)
-            if 0 < s < STEPS:
-                quantise(r_grouped, r_codes, r_scales, 0, 2)
-            if s + 2 in SORTED and s <= 1:
+                    gather_words(nc.vector.tensor_copy if i == 1 and s in () else nc.scalar.copy, x_grouped, i, bank)
+            for d in GAIN_AT.get(s, ()):
+                spread_gain(d, nc.vector.tensor_copy if s == 0 and d == 0 else nc.scalar.copy)
+            if s + 2 in SORTED:
                 sort_strain(s + 2)
+            if s >= 2:
+                quantise(*r_ops[s - 2], 0, 2)
             if s == 0:
-                rhos.append([stage_one(s, 1, h, now[0], now[1]) for h in range(2)])
-            elif s < STEPS:
-                rhos = [[stage_one(s, i, h, now[0], now[1]) for h in range(2)] for i in range(2)]
-            if s - 1 == HELD:
-                held = (r_codes, r_scales)
-            elif s == STEPS:
+                weigh(s, 0, 1)
+            if s < LAST:
+                quantise(x_grouped, x_codes, x_scales, 0, 2)
+            if s > 0:
+                for h in range(2):
+                    stage_one(s, 0, h, *x_ops[s])
+                weigh(s, 0, 1)
+            for h in range(2):
+                stage_one(s, 1, h, *x_ops[s])
+            if s >= 2 and s - 2 != HELD:
                 for i in range(2):
-                    quantise(r_grouped, r_codes, r_scales, i, i + 1)
-                for i in range(2):
-                    stage_two(HELD, i, held[0], held[1])
-                for i in range(2):
-                    stage_two(s - 1, i, r_codes, r_scales)
-            elif s > 0:
-                for i in range(2):
-                    stage_two(s - 1, i, r_codes, r_scales)
+                    stage_two(s - 2, i, *r_ops[s - 2][1:])
+
+        weigh(LAST, 1, 2)
+        for i in range(2):
+            rho_side(LAST - 1, i)
+        rho_side(LAST, 0)
+        quantise(*r_ops[LAST - 1], 0, 2)
+        for i in range(2):
+            stage_two(HELD, i, *r_ops[HELD][1:])
+        rho_side(LAST, 1)
+        for i in range(2):
+            quantise(*r_ops[LAST], i, i + 1)
+        for s in (LAST - 1, LAST):
+            for i in range(2):
+                stage_two(s, i, *r_ops[s][1:])

@@ -18,313 +18,274 @@ ALU = mybir.AluOpType
 
 P = 128
 BANK = 512
-ORDER = [(0, 0), (0, 1), (1, 0), (2, 0), (3, 0), (1, 1), (2, 1), (3, 1)]
-STEPS = len(ORDER)
+GROUPS = 2
+TILES = 2
+ROTATING = 6
+
+ORDER = [(0, 0), (0, 1)] + [(d, 0) for d in range(1, D)] + [(d, 1) for d in range(1, D)]
+LAST = len(ORDER) - 1
 HELD = 1
-ROT = 6
-GAIN_AT = {0: (0,), 1: (1,), 2: (2,), 3: (3,)}
-SORTED = (3, 4, 5, 6, 7)
-WARM = 0
+RHO_LAG = 2
+FIRST_SORTED = 3
+T_RUNS = [(0, 1), (1, 2), (2, D)]
+C_RUNS = [(0, 2), (2, D)]
 
 
 def tile_detector_template_bank_s14_kernel(tc, strain, gain, tmpl_words, tmpl_scales, cell_words, cell_scales, out):
     nc = tc.nc
+    on_scalar, on_vector = nc.scalar.copy, nc.vector.tensor_copy
     with ExitStack() as ctx:
         keep = ctx.enter_context(tc.tile_pool(name="keep", bufs=1))
         work = ctx.enter_context(tc.tile_pool(name="work", bufs=2))
         psum = ctx.enter_context(tc.psum_pool(name="psum", bufs=1))
         ctx.enter_context(tc.manual_schedule())
 
-        uses = []
+        banks_taken = []
 
         def next_bank(shape):
-            uses.append(len(uses))
-            return psum.tile(shape, F32, name="rot%d" % (uses[-1] % ROT))
+            banks_taken.append(shape)
+            return psum.tile(shape, F32, name="bank%d" % ((len(banks_taken) - 1) % ROTATING))
 
         ident = keep.tile([P, P], F32, name="ident")
         make_identity(nc, ident[:])
 
-        table_in = keep.tile([P, 8], F32, name="table_in")
-        table_out = keep.tile([P, 8], F32, name="table_out")
-
-        t_runs = [(0, 1), (1, 2), (2, 4)]
-        c_runs = [(0, 2), (2, 4)]
-        t_planes = []
-        for a, b in t_runs:
-            plane = keep.tile([P, 2 * (b - a), N], U8, name="tplane%d" % a, align_bytes=64)
-            t_planes.append(plane)
-        c_planes = []
-        for a, b in c_runs:
-            plane = keep.tile([P, 2 * (b - a), R], U8, name="cplane%d" % a, align_bytes=64)
-            c_planes.append(plane)
+        t_planes = [keep.tile([P, GROUPS * (b - a), N], U8, name="t_plane%d" % a, align_bytes=64) for a, b in T_RUNS]
+        c_planes = [keep.tile([P, GROUPS * (b - a), R], U8, name="c_plane%d" % a, align_bytes=64) for a, b in C_RUNS]
         gain_rows = keep.tile([P, BANK], BF16, name="gain_rows")
         nc.vector.memset(gain_rows[:], 0.0)
         nc.vector.memset(t_planes[0][:].bitcast(I32), 0)
+
+        table_in = keep.tile([P, 8], F32, name="table_in")
+        table_out = keep.tile([P, 8], F32, name="table_out")
         nc.vector.memset(table_in[:], 0.0)
         nc.scalar.activation(out=table_out[:], in_=table_in[:], func=ACT.Square)
-        for plane in (c_planes[0], t_planes[1], t_planes[2], c_planes[1]):
+
+        for plane in (t_planes[1], c_planes[0], t_planes[2], c_planes[1]):
             nc.vector.memset(plane[:].bitcast(I32), 0)
 
-        def load_plane(plane, scales, a, b):
-            rows = scales[2 * a : 2 * b].rearrange("g (q r) n -> r q g n", r=4)
+        x_tiles, x_loads, t_words, c_words = {}, {}, {}, {}
+
+        def load_strain(s, first=0, count=TILES):
+            d, half = ORDER[s]
+            m0 = (TILES * half + first) * P
+            x = keep.tile([P, count, K], BF16, name="x%d_%d" % (s, first))
+            nc.sync.dma_start(out=x[:], in_=strain[d, m0 : m0 + count * P, :].rearrange("(i m) k -> m i k", m=P))
+            x_loads[s] = x
+            for i in range(count):
+                x_tiles[s, first + i] = x[:, i, :]
+
+        def load_words(into, words, d, name):
+            into[d] = keep.tile([P, GROUPS, words.shape[2]], U8, name="%s%d" % (name, d), align_bytes=64)
+            groups = words[GROUPS * d : GROUPS * (d + 1)].rearrange("g p n -> p g n")
+            nc.sync.dma_start(out=into[d][:].bitcast(I32), in_=groups.bitcast(I32))
+
+        def load_plane(plane, scales, run):
+            rows = scales[GROUPS * run[0] : GROUPS * run[1]].rearrange("g (q r) n -> r q g n", r=4)
             for r in range(4):
                 nc.sync.dma_start(out=plane[r:P:32].bitcast(I32), in_=rows[r].bitcast(I32))
 
-        def t_scale(d, g, h):
-            for (a, b), plane in zip(t_runs, t_planes):
-                if a <= d < b:
-                    return plane[:, 2 * (d - a) + g, h * BANK : (h + 1) * BANK]
+        def plane_of(planes, runs, d, g):
+            j = [a <= d < b for a, b in runs].index(True)
+            return planes[j][:, GROUPS * (d - runs[j][0]) + g, :]
 
-        def c_scale(d, h):
-            for (a, b), plane in zip(c_runs, c_planes):
-                if a <= d < b:
-                    return plane[:, 2 * (d - a) + h, :]
+        for i in range(TILES):
+            load_strain(0, i, 1)
+        load_words(t_words, tmpl_words, 0, "t")
+        nc.sync.dma_start(out=gain_rows[0 : GROUPS * D, :], in_=gain.rearrange("d (g n) -> (d g) n", g=GROUPS))
+        load_plane(t_planes[0], tmpl_scales, T_RUNS[0])
+        for i in range(TILES):
+            load_strain(1, i, 1)
+        load_strain(2)
+        load_strain(3)
+        load_plane(t_planes[1], tmpl_scales, T_RUNS[1])
+        load_words(t_words, tmpl_words, 1, "t")
+        load_strain(4)
+        load_plane(c_planes[0], cell_scales, C_RUNS[0])
+        load_words(c_words, cell_words, 0, "c")
+        load_plane(t_planes[2], tmpl_scales, T_RUNS[2])
+        load_plane(c_planes[1], cell_scales, C_RUNS[1])
+        for d in range(1, D):
+            if d + 1 < D:
+                load_words(t_words, tmpl_words, d + 1, "t")
+            load_words(c_words, cell_words, d, "c")
+            load_strain(4 + d)
 
-        x_tiles = {}
-        x_whole = {}
-        t_tiles = {}
-        c_tiles = {}
-
-        def load_x(s, i0, i1):
-            d, pair = ORDER[s]
-            rows = strain[d, (2 * pair + i0) * P : (2 * pair + i1) * P, :]
-            x = keep.tile([P, i1 - i0, K], BF16, name="x%d_%d" % (s, i0))
-            nc.sync.dma_start(out=x[:], in_=rows.rearrange("(i m) k -> m i k", m=P))
-            x_whole[s] = x
-            for i in range(i0, i1):
-                x_tiles[s, i] = x[:, i - i0, :]
-
-        def load_t(d):
-            w = keep.tile([P, 2, 2 * N], U8, name="t%d" % d, align_bytes=64)
-            nc.sync.dma_start(out=w[:].bitcast(I32), in_=tmpl_words[2 * d : 2 * d + 2].rearrange("g p n -> p g n").bitcast(I32))
-            t_tiles[d] = w
-
-        def load_c(d):
-            w = keep.tile([P, 2, 2 * R], U8, name="c%d" % d, align_bytes=64)
-            nc.sync.dma_start(out=w[:].bitcast(I32), in_=cell_words[2 * d : 2 * d + 2].rearrange("g p n -> p g n").bitcast(I32))
-            c_tiles[d] = w
-
-        def load_gain():
-            nc.sync.dma_start(out=gain_rows[0 : 2 * D, :], in_=gain.rearrange("d (h n) -> (d h) n", h=2))
-
-        load_x(0, 0, 1)
-        load_x(0, 1, 2)
-        load_t(0)
-        load_gain()
-        load_plane(t_planes[0], tmpl_scales, *t_runs[0])
-        load_x(1, 0, 1)
-        load_x(1, 1, 2)
-        load_x(2, 0, 2)
-        load_x(3, 0, 2)
-        load_plane(t_planes[1], tmpl_scales, *t_runs[1])
-        load_t(1)
-        load_x(4, 0, 2)
-        load_plane(c_planes[0], cell_scales, *c_runs[0])
-        load_c(0)
-        load_plane(t_planes[2], tmpl_scales, *t_runs[2])
-        load_plane(c_planes[1], cell_scales, *c_runs[1])
-        load_t(2)
-        load_c(1)
-        load_x(5, 0, 2)
-        load_t(3)
-        load_c(2)
-        load_x(6, 0, 2)
-        load_c(3)
-        load_x(7, 0, 2)
-
+        gain_cols = keep.tile([P, 2 * GROUPS * D], F32, name="gain_cols")
         gains = {}
-        gain_cols = keep.tile([P, 4 * D], F32, name="gain_cols")
 
         def turn_gain():
             bank = next_bank([P, 2, P])
             for u in range(2):
                 nc.tensor.transpose(bank[:, u, :], gain_rows[:].bitcast(F32)[:, u : 2 * P : 2], ident[:])
-            nc.vector.tensor_copy(
+            on_vector(
                 out=gain_cols[:].rearrange("p (j u) -> p j u", u=2),
-                in_=bank[:, :, 0 : 2 * D].rearrange("p u j -> p j u"),
+                in_=bank[:, :, 0 : GROUPS * D].rearrange("p u j -> p j u"),
             )
 
         def spread_gain(d, copy):
-            words = gain_cols[:]
-            bank = next_bank([P, 4, P])
-            for j in range(4):
-                nc.tensor.transpose(bank[:, j, :], words[:, 4 * d + j : 4 * d + j + 1].to_broadcast([P, P]), ident[:])
+            bank = next_bank([P, 2 * GROUPS, P])
+            for j in range(2 * GROUPS):
+                col = 2 * GROUPS * d + j
+                nc.tensor.transpose(bank[:, j, :], gain_cols[:, col : col + 1].to_broadcast([P, P]), ident[:])
             gains[d] = keep.tile([P, N], BF16, name="gain%d" % d)
             copy(out=gains[d][:].bitcast(F32), in_=bank[:].rearrange("p j q -> p (j q)"))
 
-        sorted_x = {}
-        squares = {}
-        rhos = {}
+        x_sorted, squares, rhos, x_ops, rho_ops = {}, {}, {}, {}, {}
 
-        def sort_strain(s):
-            tidy = work.tile([P, 2 * BANK], F32, name="tidy")
-            nc.vector.tensor_copy(
-                out=tidy[:].rearrange("p (j u q) -> p j u q", j=4, u=2),
-                in_=x_whole[s][:].rearrange("p i k -> p (i k)").bitcast(F32).rearrange("p (j q u) -> p j u q", j=4, u=2),
-            )
-            for i in range(2):
-                sorted_x[s, i] = tidy[:, i * BANK : (i + 1) * BANK]
-
-        def turn_strain(s, i):
-            bank = next_bank([P, 4, P])
-            for g in range(2):
-                for u in range(2):
-                    if s in SORTED:
-                        src = sorted_x[s, i][:, (2 * g + u) * P : (2 * g + u + 1) * P]
-                    else:
-                        src = x_tiles[s, i].bitcast(F32)[:, 2 * P * g + u : 2 * P * (g + 1) : 2]
-                    nc.tensor.transpose(bank[:, 2 * g + u, :], src, ident[:])
-            return bank
-
-        def turn_rho(s, i):
-            words = rhos[s, i][:].bitcast(F32)
-            bank = next_bank([P, 4, P])
-            for j in range(4):
-                nc.tensor.transpose(bank[:, j, :], words[:, j * P : (j + 1) * P], ident[:])
-            return bank
-
-        def gather_words(copy, grouped, i, bank):
-            dst = grouped[:].bitcast(F32)[:, i * BANK : (i + 1) * BANK]
-            copy(out=dst.rearrange("p (g m u) -> p g m u", g=2, u=2), in_=bank[:].rearrange("p (g u) m -> p g m u", u=2))
-
-        def quantise(grouped, codes, scales, i0, i1):
-            nc.vector.quantize_mx(
-                out=codes[:, i0 * 2 * P : i1 * 2 * P].bitcast(FP8X4),
-                scales=scales[:, i0 * 2 * P : i1 * 2 * P],
-                in_=grouped[:, i0 * 2 * BANK : i1 * 2 * BANK],
-            )
-
-        def new_operand(name, tag):
-            grouped = work.tile([P, 4 * BANK], BF16, name=name + "_grouped", align_bytes=64)
-            codes = work.tile([P, BANK], U32, name=tag + "_codes", align_bytes=64)
-            scales = work.tile([P, BANK], U8, name=tag + "_scales", align_bytes=64)
+        def new_operand(kind, tag):
+            grouped = work.tile([P, TILES * K], BF16, name=kind + "_grouped", align_bytes=64)
+            codes = work.tile([P, TILES * GROUPS * P], U32, name=tag + "_codes", align_bytes=64)
+            scales = work.tile([P, TILES * GROUPS * P], U8, name=tag + "_scales", align_bytes=64)
             return grouped, codes, scales
 
-        def stage_one(s, i, h, codes, scales):
-            d = ORDER[s][0]
-            z = next_bank([P, BANK])
-            for g in range(2):
-                cols = slice((2 * i + g) * P, (2 * i + g + 1) * P)
-                nc.tensor.matmul_mx(
-                    out=z[:],
-                    lhsT=codes[:, cols].bitcast(FP8X4),
-                    lhsT_scale=scales[:, cols],
-                    rhs=t_tiles[d][:, g, h * 2 * BANK : (h + 1) * 2 * BANK].bitcast(FP4X4),
-                    rhs_scale=t_scale(d, g, h),
-                    start=(g == 0),
-                    stop=(g == 1),
-                )
-            if h == 0:
-                squares[s, i] = work.tile([P, N], F32, name="squared", bufs=3)
-            nc.scalar.activation(
-                out=squares[s, i][:, h * BANK : (h + 1) * BANK].rearrange("p (u q e) -> p u q e", u=2, e=2),
-                in_=z[:].rearrange("p (q u e) -> p u q e", u=2, e=2),
-                func=ACT.Square,
+        def sort_strain(s):
+            x_sorted[s] = work.tile([P, TILES * BANK], F32, name="x_sorted")
+            pairs = x_loads[s][:].rearrange("m i k -> m (i k)").bitcast(F32)
+            on_vector(
+                out=x_sorted[s][:].rearrange("m (j u q) -> m j u q", j=TILES * GROUPS, u=2),
+                in_=pairs.rearrange("m (j q u) -> m j u q", j=TILES * GROUPS, u=2),
             )
 
-        def weigh(s, i, parts):
+        def turn(columns, operand, i, copy):
+            bank = next_bank([P, 2 * GROUPS, P])
+            for g in range(GROUPS):
+                for u in range(2):
+                    nc.tensor.transpose(bank[:, 2 * g + u, :], columns(g, u), ident[:])
+            pairs = operand[0][:].bitcast(F32)[:, i * BANK : (i + 1) * BANK]
+            copy(
+                out=pairs.rearrange("p (g m u) -> p g m u", g=GROUPS, u=2),
+                in_=bank[:].rearrange("p (g u) m -> p g m u", u=2),
+            )
+
+        def sorted_columns(pairs):
+            return lambda g, u: pairs[:, (2 * g + u) * P : (2 * g + u + 1) * P]
+
+        def turn_strain(s, i):
+            if i == 0:
+                x_ops[s] = new_operand("x", "x")
+            if s >= FIRST_SORTED:
+                columns = sorted_columns(x_sorted[s][:, i * BANK : (i + 1) * BANK])
+            else:
+                pairs = x_tiles[s, i].bitcast(F32)
+                columns = lambda g, u: pairs[:, 2 * P * g + u : 2 * P * (g + 1) : 2]
+            turn(columns, x_ops[s], i, on_scalar)
+
+        def turn_rho(s, i, copy):
+            if i == 0:
+                rho_ops[s] = new_operand("rho", "held" if s == HELD else "rho")
+            turn(sorted_columns(rhos[s, i][:].bitcast(F32)), rho_ops[s], i, copy)
+
+        def quantise(operand, first=0, count=TILES):
+            grouped, codes, scales = operand
+            cols = slice(first * GROUPS * P, (first + count) * GROUPS * P)
+            nc.vector.quantize_mx(
+                out=codes[:, cols].bitcast(FP8X4), scales=scales[:, cols], in_=grouped[:, first * K : (first + count) * K]
+            )
+
+        def mx_pass(acc, operand, i, g, words, plane, start, stop):
+            cols = slice((GROUPS * i + g) * P, (GROUPS * i + g + 1) * P)
+            nc.tensor.matmul_mx(
+                out=acc[:],
+                lhsT=operand[1][:, cols].bitcast(FP8X4),
+                lhsT_scale=operand[2][:, cols],
+                rhs=words.bitcast(FP4X4),
+                rhs_scale=plane,
+                start=start,
+                stop=stop,
+            )
+
+        def first_stage(s, i):
             d = ORDER[s][0]
-            rhos[s, i] = work.tile([P, N], BF16, name="rho", bufs=6)
-            for c0 in range(0, N, N // parts):
-                cols = slice(c0, c0 + N // parts)
-                nc.vector.tensor_tensor(out=rhos[s, i][:, cols], in0=squares[s, i][:, cols], in1=gains[d][:, cols], op=ALU.mult)
-
-        sums = {}
-        added = {}
-
-        def stage_two(s, i, codes, scales):
-            d, pair = ORDER[s]
-            done = added.get((pair, i), 0)
-            added[pair, i] = done + 1
-            if done == 0:
-                sums[i] = psum.tile([P, R], F32, name="sum%d" % i)
-            for h in range(2):
-                cols = slice((2 * i + h) * P, (2 * i + h + 1) * P)
-                nc.tensor.matmul_mx(
-                    out=sums[i][:],
-                    lhsT=codes[:, cols].bitcast(FP8X4),
-                    lhsT_scale=scales[:, cols],
-                    rhs=c_tiles[d][:, h, :].bitcast(FP4X4),
-                    rhs_scale=c_scale(d, h),
-                    start=(done == 0 and h == 0),
-                    stop=(done == D - 1 and h == 1),
+            for h in range(GROUPS):
+                z = next_bank([P, BANK])
+                for g in range(GROUPS):
+                    words = t_words[d][:, g, 2 * h * BANK : 2 * (h + 1) * BANK]
+                    plane = plane_of(t_planes, T_RUNS, d, g)[:, h * BANK : (h + 1) * BANK]
+                    mx_pass(z, x_ops[s], i, g, words, plane, g == 0, g == GROUPS - 1)
+                if h == 0:
+                    squares[s, i] = work.tile([P, N], F32, name="squares", bufs=2 * TILES)
+                nc.scalar.activation(
+                    out=squares[s, i][:, h * BANK : (h + 1) * BANK].rearrange("m (u q e) -> m u q e", u=2, e=2),
+                    in_=z[:].rearrange("m (q u e) -> m u q e", u=2, e=2),
+                    func=ACT.Square,
                 )
-            if done == D - 1:
-                m0 = (2 * pair + i) * P
-                if pair == 1 and i == 1:
-                    for c0 in (0, R // 2):
-                        half = work.tile([P, R // 2], F32, name="half")
-                        nc.scalar.copy(out=half[:], in_=sums[i][:, c0 : c0 + R // 2])
-                        nc.sync.dma_start(out=out[m0 : m0 + P, c0 : c0 + R // 2], in_=half[:])
-                else:
-                    result = work.tile([P, R], F32, name="result")
-                    (nc.vector.tensor_copy if pair == 1 else nc.scalar.copy)(out=result[:], in_=sums[i][:])
-                    nc.sync.dma_start(out=out[m0 : m0 + P, :], in_=result[:])
 
-        x_grouped, x_codes, x_scales = new_operand("x", "x")
-        bank = turn_strain(0, 0)
-        gather_words(nc.scalar.copy, x_grouped, 0, bank)
-        quantise(x_grouped, x_codes, x_scales, 0, 1)
-        bank = turn_strain(0, 1)
-        gather_words(nc.scalar.copy, x_grouped, 1, bank)
-        quantise(x_grouped, x_codes, x_scales, 1, 2)
+        def weigh(s, i, width=N):
+            rhos[s, i] = work.tile([P, N], BF16, name="rho", bufs=TILES * (RHO_LAG + 1))
+            for c0 in range(0, N, width):
+                cols = slice(c0, c0 + width)
+                nc.vector.tensor_tensor(
+                    out=rhos[s, i][:, cols], in0=squares[s, i][:, cols], in1=gains[ORDER[s][0]][:, cols], op=ALU.mult
+                )
+
+        sums, added = {}, {}
+
+        def second_stage(s, i):
+            d, half = ORDER[s]
+            before = added.get((half, i), 0)
+            added[half, i] = before + 1
+            if before == 0:
+                sums[i] = psum.tile([P, R], F32, name="sum%d" % i)
+            for g in range(GROUPS):
+                start, stop = before == 0 and g == 0, before == D - 1 and g == GROUPS - 1
+                mx_pass(sums[i], rho_ops[s], i, g, c_words[d][:, g, :], plane_of(c_planes, C_RUNS, d, g), start, stop)
+
+        def store(half, i, copy, width=R):
+            m0 = (TILES * half + i) * P
+            for c0 in range(0, R, width):
+                result = work.tile([P, width], F32, name="result%d" % width)
+                copy(out=result[:], in_=sums[i][:, c0 : c0 + width])
+                nc.sync.dma_start(out=out[m0 : m0 + P, c0 : c0 + width], in_=result[:])
+
+        for i in range(TILES):
+            turn_strain(0, i)
+            quantise(x_ops[0], i, 1)
         turn_gain()
 
-        x_ops = {0: (x_codes, x_scales)}
-        r_ops = {}
-        LAST = STEPS - 1
-
-        def rho_side(s, i):
-            if i == 0:
-                r_ops[s] = new_operand("r", "held" if s == HELD else "r")
-            bank = turn_rho(s, i)
-            gather_words(nc.scalar.copy if i == 0 or s in (6, 7) else nc.vector.tensor_copy, r_ops[s][0], i, bank)
-
-        for s in range(STEPS):
-            if s > 0:
-                weigh(s - 1, 1, 1)
+        for s in range(LAST + 1):
+            old = s - RHO_LAG
             if s == 0:
-                for h in range(2):
-                    stage_one(s, 0, h, *x_ops[s])
-            if s >= 2:
-                for i in range(2):
-                    rho_side(s - 2, i)
+                first_stage(0, 0)
+            if old >= 0:
+                turn_rho(old, 0, on_scalar)
+                turn_rho(old, 1, on_vector)
             if s < LAST:
-                x_grouped, x_codes, x_scales = new_operand("x", "x")
-                x_ops[s + 1] = (x_codes, x_scales)
-                for i in range(2):
-                    bank = turn_strain(s + 1, i)
-                    gather_words(nc.vector.tensor_copy if i == 1 and s in () else nc.scalar.copy, x_grouped, i, bank)
-            for d in GAIN_AT.get(s, ()):
-                spread_gain(d, nc.vector.tensor_copy if s == 0 and d == 0 else nc.scalar.copy)
-            if s + 2 in SORTED:
+                for i in range(TILES):
+                    turn_strain(s + 1, i)
+            if s < D:
+                spread_gain(s, on_vector if s == 0 else on_scalar)
+            if s == LAST:
+                for i in range(TILES):
+                    store(0, i, on_scalar)
+            if FIRST_SORTED <= s + 2 <= LAST:
                 sort_strain(s + 2)
-            if s >= 2:
-                quantise(*r_ops[s - 2], 0, 2)
-            if s == 0:
-                weigh(s, 0, 1)
-            if s < LAST:
-                quantise(x_grouped, x_codes, x_scales, 0, 2)
+            if old >= 0:
+                quantise(rho_ops[old])
             if s > 0:
-                for h in range(2):
-                    stage_one(s, 0, h, *x_ops[s])
-                weigh(s, 0, 1)
-            for h in range(2):
-                stage_one(s, 1, h, *x_ops[s])
-            if s >= 2 and s - 2 != HELD:
-                for i in range(2):
-                    stage_two(s - 2, i, *r_ops[s - 2][1:])
+                weigh(s - 1, 1)
+            if s < LAST:
+                quantise(x_ops[s + 1])
+            if s > 0:
+                first_stage(s, 0)
+            weigh(s, 0)
+            first_stage(s, 1)
+            if old >= 0 and old != HELD:
+                for i in range(TILES):
+                    second_stage(old, i)
 
-        weigh(LAST, 1, 2)
-        for i in range(2):
-            rho_side(LAST - 1, i)
-        rho_side(LAST, 0)
-        quantise(*r_ops[LAST - 1], 0, 2)
-        for i in range(2):
-            stage_two(HELD, i, *r_ops[HELD][1:])
-        rho_side(LAST, 1)
-        for i in range(2):
-            quantise(*r_ops[LAST], i, i + 1)
-        for s in (LAST - 1, LAST):
-            for i in range(2):
-                stage_two(s, i, *r_ops[s][1:])
+        weigh(LAST, 1, BANK)
+        for i in range(TILES):
+            turn_rho(LAST - 1, i, on_scalar)
+        turn_rho(LAST, 0, on_scalar)
+        quantise(rho_ops[LAST - 1])
+        for i in range(TILES):
+            second_stage(HELD, i)
+        turn_rho(LAST, 1, on_scalar)
+        for i in range(TILES):
+            quantise(rho_ops[LAST], i, 1)
+        for i in range(TILES):
+            second_stage(LAST - 1, i)
+        second_stage(LAST, 0)
+        store(1, 0, on_vector)
+        second_stage(LAST, 1)
+        store(1, 1, on_scalar, R // 2)

@@ -29,6 +29,7 @@ RHO_LAG = 2
 FIRST_SORTED = 3
 T_RUNS = [(0, 1), (1, 2), (2, D)]
 C_RUNS = [(0, 2), (2, D)]
+WARM_BEFORE, WARM_BETWEEN = 3, 2
 
 
 def tile_detector_template_bank_s14_kernel(tc, strain, gain, tmpl_words, tmpl_scales, cell_words, cell_scales, out):
@@ -49,6 +50,16 @@ def tile_detector_template_bank_s14_kernel(tc, strain, gain, tmpl_words, tmpl_sc
         ident = keep.tile([P, P], F32, name="ident")
         make_identity(nc, ident[:])
 
+        zeros = keep.tile([P, BANK], BF16, name="zeros")
+        nc.vector.memset(zeros[:], 0.0)
+        idle_bank = psum.tile([P, BANK], F32, name="sum0")
+
+        def warm_up(count):
+            for j in range(count):
+                nc.tensor.matmul(idle_bank[:], lhsT=zeros[:, 0:P], rhs=zeros[:], start=True, stop=True)
+
+        warm_up(WARM_BEFORE)
+
         t_planes = [keep.tile([P, GROUPS * (b - a), N], U8, name="t_plane%d" % a, align_bytes=64) for a, b in T_RUNS]
         c_planes = [keep.tile([P, GROUPS * (b - a), R], U8, name="c_plane%d" % a, align_bytes=64) for a, b in C_RUNS]
         gain_rows = keep.tile([P, BANK], BF16, name="gain_rows")
@@ -58,7 +69,6 @@ def tile_detector_template_bank_s14_kernel(tc, strain, gain, tmpl_words, tmpl_sc
         table_in = keep.tile([P, 8], F32, name="table_in")
         table_out = keep.tile([P, 8], F32, name="table_out")
         nc.vector.memset(table_in[:], 0.0)
-        nc.scalar.activation(out=table_out[:], in_=table_in[:], func=ACT.Square)
 
         for plane in (t_planes[1], c_planes[0], t_planes[2], c_planes[1]):
             nc.vector.memset(plane[:].bitcast(I32), 0)
@@ -74,10 +84,17 @@ def tile_detector_template_bank_s14_kernel(tc, strain, gain, tmpl_words, tmpl_sc
             for i in range(count):
                 x_tiles[s, first + i] = x[:, i, :]
 
-        def load_words(into, words, d, name):
-            into[d] = keep.tile([P, GROUPS, words.shape[2]], U8, name="%s%d" % (name, d), align_bytes=64)
-            groups = words[GROUPS * d : GROUPS * (d + 1)].rearrange("g p n -> p g n")
-            nc.sync.dma_start(out=into[d][:].bitcast(I32), in_=groups.bitcast(I32))
+        def load_cells(d):
+            c_words[d] = keep.tile([P, GROUPS, 2 * R], U8, name="c%d" % d, align_bytes=64)
+            groups = cell_words[GROUPS * d : GROUPS * (d + 1)].rearrange("g p n -> p g n")
+            nc.sync.dma_start(out=c_words[d][:].bitcast(I32), in_=groups.bitcast(I32))
+
+        def load_templates(d, first=0, count=GROUPS):
+            w = keep.tile([P, GROUPS, count * 2 * BANK], U8, name="t%d_%d" % (d, first), align_bytes=64)
+            groups = tmpl_words[GROUPS * d : GROUPS * (d + 1)].rearrange("g p n -> p g n")
+            nc.sync.dma_start(out=w[:].bitcast(I32), in_=groups[:, :, first * 2 * BANK : (first + count) * 2 * BANK].bitcast(I32))
+            for h in range(count):
+                t_words[d, first + h] = w[:, :, h * 2 * BANK : (h + 1) * 2 * BANK]
 
         def load_plane(plane, scales, run):
             rows = scales[GROUPS * run[0] : GROUPS * run[1]].rearrange("g (q r) n -> r q g n", r=4)
@@ -88,26 +105,28 @@ def tile_detector_template_bank_s14_kernel(tc, strain, gain, tmpl_words, tmpl_sc
             j = [a <= d < b for a, b in runs].index(True)
             return planes[j][:, GROUPS * (d - runs[j][0]) + g, :]
 
-        for i in range(TILES):
-            load_strain(0, i, 1)
-        load_words(t_words, tmpl_words, 0, "t")
-        nc.sync.dma_start(out=gain_rows[0 : GROUPS * D, :], in_=gain.rearrange("d (g n) -> (d g) n", g=GROUPS))
+        load_strain(0, 0, 1)
+        load_templates(0, 0, 1)
+        nc.scalar.dma_start(out=gain_rows[0 : GROUPS * D, :], in_=gain.rearrange("d (g n) -> (d g) n", g=GROUPS))
+        nc.scalar.activation(out=table_out[:], in_=table_in[:], func=ACT.Square)
         load_plane(t_planes[0], tmpl_scales, T_RUNS[0])
+        load_strain(0, 1, 1)
+        load_templates(0, 1, 1)
         for i in range(TILES):
             load_strain(1, i, 1)
         load_strain(2)
         load_strain(3)
         load_plane(t_planes[1], tmpl_scales, T_RUNS[1])
-        load_words(t_words, tmpl_words, 1, "t")
+        load_templates(1)
         load_strain(4)
         load_plane(c_planes[0], cell_scales, C_RUNS[0])
-        load_words(c_words, cell_words, 0, "c")
+        load_cells(0)
         load_plane(t_planes[2], tmpl_scales, T_RUNS[2])
         load_plane(c_planes[1], cell_scales, C_RUNS[1])
         for d in range(1, D):
             if d + 1 < D:
-                load_words(t_words, tmpl_words, d + 1, "t")
-            load_words(c_words, cell_words, d, "c")
+                load_templates(d + 1)
+            load_cells(d)
             load_strain(4 + d)
 
         gain_cols = keep.tile([P, 2 * GROUPS * D], F32, name="gain_cols")
@@ -199,7 +218,7 @@ def tile_detector_template_bank_s14_kernel(tc, strain, gain, tmpl_words, tmpl_sc
             for h in range(GROUPS):
                 z = next_bank([P, BANK])
                 for g in range(GROUPS):
-                    words = t_words[d][:, g, 2 * h * BANK : 2 * (h + 1) * BANK]
+                    words = t_words[d, h][:, g, :]
                     plane = plane_of(t_planes, T_RUNS, d, g)[:, h * BANK : (h + 1) * BANK]
                     mx_pass(z, x_ops[s], i, g, words, plane, g == 0, g == GROUPS - 1)
                 if h == 0:
@@ -237,23 +256,26 @@ def tile_detector_template_bank_s14_kernel(tc, strain, gain, tmpl_words, tmpl_sc
                 copy(out=result[:], in_=sums[i][:, c0 : c0 + width])
                 nc.sync.dma_start(out=out[m0 : m0 + P, c0 : c0 + width], in_=result[:])
 
-        for i in range(TILES):
-            turn_strain(0, i)
-            quantise(x_ops[0], i, 1)
+        turn_strain(0, 0)
         turn_gain()
+        quantise(x_ops[0], 0, 1)
+        warm_up(WARM_BETWEEN)
+        for d in range(D - 1):
+            spread_gain(d, on_vector if d % 2 == 0 else on_scalar)
+        turn_strain(0, 1)
+        first_stage(0, 0)
+        quantise(x_ops[0], 1, 1)
+        spread_gain(D - 1, on_vector)
+        weigh(0, 0)
 
         for s in range(LAST + 1):
             old = s - RHO_LAG
-            if s == 0:
-                first_stage(0, 0)
             if old >= 0:
                 turn_rho(old, 0, on_scalar)
                 turn_rho(old, 1, on_vector)
             if s < LAST:
                 for i in range(TILES):
                     turn_strain(s + 1, i)
-            if s < D:
-                spread_gain(s, on_vector if s == 0 else on_scalar)
             if s == LAST:
                 for i in range(TILES):
                     store(0, i, on_scalar)
@@ -267,7 +289,7 @@ def tile_detector_template_bank_s14_kernel(tc, strain, gain, tmpl_words, tmpl_sc
                 quantise(x_ops[s + 1])
             if s > 0:
                 first_stage(s, 0)
-            weigh(s, 0)
+                weigh(s, 0)
             first_stage(s, 1)
             if old >= 0 and old != HELD:
                 for i in range(TILES):

from contextlib import ExitStack

import concourse.mybir as mybir
from concourse.masks import make_identity

D, M, K, N, R = 4, 512, 1024, 1024, 512
FLOPS = 2 * D * M * K * N + 2 * D * M * N * R

F32 = mybir.dt.float32
BF16 = mybir.dt.bfloat16
I32 = mybir.dt.int32
U32 = mybir.dt.uint32
U8 = mybir.dt.uint8
FP8X4 = mybir.dt.float8_e4m3fn_x4
FP4X4 = mybir.dt.float4_e2m1fn_x4
ACT = mybir.ActivationFunctionType
ALU = mybir.AluOpType

P = 128
BANK = 512
GROUPS = 2
TILES = 2
ROTATING = 6

ORDER = [(0, 0), (0, 1)] + [(d, 0) for d in range(1, D)] + [(d, 1) for d in range(1, D)]
LAST = len(ORDER) - 1
HELD = 1
RHO_LAG = 2
FIRST_SORTED = 3
T_RUNS = [(0, 1), (1, 2), (2, D)]
C_RUNS = [(0, 2), (2, D)]
WARM_BEFORE, WARM_BETWEEN = 3, 2


def tile_detector_template_bank_s14_kernel(tc, strain, gain, tmpl_words, tmpl_scales, cell_words, cell_scales, out):
    nc = tc.nc
    on_scalar, on_vector = nc.scalar.copy, nc.vector.tensor_copy
    with ExitStack() as ctx:
        keep = ctx.enter_context(tc.tile_pool(name="keep", bufs=1))
        work = ctx.enter_context(tc.tile_pool(name="work", bufs=2))
        psum = ctx.enter_context(tc.psum_pool(name="psum", bufs=1))
        ctx.enter_context(tc.manual_schedule())

        banks_taken = []

        def next_bank(shape):
            banks_taken.append(shape)
            return psum.tile(shape, F32, name="bank%d" % ((len(banks_taken) - 1) % ROTATING))

        ident = keep.tile([P, P], F32, name="ident")
        make_identity(nc, ident[:])

        zeros = keep.tile([P, BANK], BF16, name="zeros")
        nc.vector.memset(zeros[:], 0.0)
        idle_bank = psum.tile([P, BANK], F32, name="sum0")

        def warm_up(count):
            for j in range(count):
                nc.tensor.matmul(idle_bank[:], lhsT=zeros[:, 0:P], rhs=zeros[:], start=True, stop=True)

        warm_up(WARM_BEFORE)

        t_planes = [keep.tile([P, GROUPS * (b - a), N], U8, name="t_plane%d" % a, align_bytes=64) for a, b in T_RUNS]
        c_planes = [keep.tile([P, GROUPS * (b - a), R], U8, name="c_plane%d" % a, align_bytes=64) for a, b in C_RUNS]
        gain_rows = keep.tile([P, BANK], BF16, name="gain_rows")
        nc.vector.memset(gain_rows[:], 0.0)
        nc.vector.memset(t_planes[0][:].bitcast(I32), 0)

        table_in = keep.tile([P, 8], F32, name="table_in")
        table_out = keep.tile([P, 8], F32, name="table_out")
        nc.vector.memset(table_in[:], 0.0)

        for plane in (t_planes[1], c_planes[0], t_planes[2], c_planes[1]):
            nc.vector.memset(plane[:].bitcast(I32), 0)

        x_tiles, x_loads, t_words, c_words = {}, {}, {}, {}

        def load_strain(s, first=0, count=TILES):
            d, half = ORDER[s]
            m0 = (TILES * half + first) * P
            x = keep.tile([P, count, K], BF16, name="x%d_%d" % (s, first))
            nc.sync.dma_start(out=x[:], in_=strain[d, m0 : m0 + count * P, :].rearrange("(i m) k -> m i k", m=P))
            x_loads[s] = x
            for i in range(count):
                x_tiles[s, first + i] = x[:, i, :]

        def load_cells(d):
            c_words[d] = keep.tile([P, GROUPS, 2 * R], U8, name="c%d" % d, align_bytes=64)
            groups = cell_words[GROUPS * d : GROUPS * (d + 1)].rearrange("g p n -> p g n")
            nc.sync.dma_start(out=c_words[d][:].bitcast(I32), in_=groups.bitcast(I32))

        def load_templates(d, first=0, count=GROUPS):
            w = keep.tile([P, GROUPS, count * 2 * BANK], U8, name="t%d_%d" % (d, first), align_bytes=64)
            groups = tmpl_words[GROUPS * d : GROUPS * (d + 1)].rearrange("g p n -> p g n")
            nc.sync.dma_start(out=w[:].bitcast(I32), in_=groups[:, :, first * 2 * BANK : (first + count) * 2 * BANK].bitcast(I32))
            for h in range(count):
                t_words[d, first + h] = w[:, :, h * 2 * BANK : (h + 1) * 2 * BANK]

        def load_plane(plane, scales, run):
            rows = scales[GROUPS * run[0] : GROUPS * run[1]].rearrange("g (q r) n -> r q g n", r=4)
            for r in range(4):
                nc.sync.dma_start(out=plane[r:P:32].bitcast(I32), in_=rows[r].bitcast(I32))

        def plane_of(planes, runs, d, g):
            j = [a <= d < b for a, b in runs].index(True)
            return planes[j][:, GROUPS * (d - runs[j][0]) + g, :]

        load_strain(0, 0, 1)
        load_templates(0, 0, 1)
        nc.scalar.dma_start(out=gain_rows[0 : GROUPS * D, :], in_=gain.rearrange("d (g n) -> (d g) n", g=GROUPS))
        nc.scalar.activation(out=table_out[:], in_=table_in[:], func=ACT.Square)
        load_plane(t_planes[0], tmpl_scales, T_RUNS[0])
        load_strain(0, 1, 1)
        load_templates(0, 1, 1)
        for i in range(TILES):
            load_strain(1, i, 1)
        load_strain(2)
        load_strain(3)
        load_plane(t_planes[1], tmpl_scales, T_RUNS[1])
        load_templates(1)
        load_strain(4)
        load_plane(c_planes[0], cell_scales, C_RUNS[0])
        load_cells(0)
        load_plane(t_planes[2], tmpl_scales, T_RUNS[2])
        load_plane(c_planes[1], cell_scales, C_RUNS[1])
        for d in range(1, D):
            if d + 1 < D:
                load_templates(d + 1)
            load_cells(d)
            load_strain(4 + d)

        gain_cols = keep.tile([P, 2 * GROUPS * D], F32, name="gain_cols")
        gains = {}

        def turn_gain():
            bank = next_bank([P, 2, P])
            for u in range(2):
                nc.tensor.transpose(bank[:, u, :], gain_rows[:].bitcast(F32)[:, u : 2 * P : 2], ident[:])
            on_vector(
                out=gain_cols[:].rearrange("p (j u) -> p j u", u=2),
                in_=bank[:, :, 0 : GROUPS * D].rearrange("p u j -> p j u"),
            )

        def spread_gain(d, copy):
            bank = next_bank([P, 2 * GROUPS, P])
            for j in range(2 * GROUPS):
                col = 2 * GROUPS * d + j
                nc.tensor.transpose(bank[:, j, :], gain_cols[:, col : col + 1].to_broadcast([P, P]), ident[:])
            gains[d] = keep.tile([P, N], BF16, name="gain%d" % d)
            copy(out=gains[d][:].bitcast(F32), in_=bank[:].rearrange("p j q -> p (j q)"))

        x_sorted, squares, rhos, x_ops, rho_ops = {}, {}, {}, {}, {}

        def new_operand(kind, tag):
            grouped = work.tile([P, TILES * K], BF16, name=kind + "_grouped", align_bytes=64)
            codes = work.tile([P, TILES * GROUPS * P], U32, name=tag + "_codes", align_bytes=64)
            scales = work.tile([P, TILES * GROUPS * P], U8, name=tag + "_scales", align_bytes=64)
            return grouped, codes, scales

        def sort_strain(s):
            x_sorted[s] = work.tile([P, TILES * BANK], F32, name="x_sorted")
            pairs = x_loads[s][:].rearrange("m i k -> m (i k)").bitcast(F32)
            on_vector(
                out=x_sorted[s][:].rearrange("m (j u q) -> m j u q", j=TILES * GROUPS, u=2),
                in_=pairs.rearrange("m (j q u) -> m j u q", j=TILES * GROUPS, u=2),
            )

        def turn(columns, operand, i, copy):
            bank = next_bank([P, 2 * GROUPS, P])
            for g in range(GROUPS):
                for u in range(2):
                    nc.tensor.transpose(bank[:, 2 * g + u, :], columns(g, u), ident[:])
            pairs = operand[0][:].bitcast(F32)[:, i * BANK : (i + 1) * BANK]
            copy(
                out=pairs.rearrange("p (g m u) -> p g m u", g=GROUPS, u=2),
                in_=bank[:].rearrange("p (g u) m -> p g m u", u=2),
            )

        def sorted_columns(pairs):
            return lambda g, u: pairs[:, (2 * g + u) * P : (2 * g + u + 1) * P]

        def turn_strain(s, i):
            if i == 0:
                x_ops[s] = new_operand("x", "x")
            if s >= FIRST_SORTED:
                columns = sorted_columns(x_sorted[s][:, i * BANK : (i + 1) * BANK])
            else:
                pairs = x_tiles[s, i].bitcast(F32)
                columns = lambda g, u: pairs[:, 2 * P * g + u : 2 * P * (g + 1) : 2]
            turn(columns, x_ops[s], i, on_scalar)

        def turn_rho(s, i, copy):
            if i == 0:
                rho_ops[s] = new_operand("rho", "held" if s == HELD else "rho")
            turn(sorted_columns(rhos[s, i][:].bitcast(F32)), rho_ops[s], i, copy)

        def quantise(operand, first=0, count=TILES):
            grouped, codes, scales = operand
            cols = slice(first * GROUPS * P, (first + count) * GROUPS * P)
            nc.vector.quantize_mx(
                out=codes[:, cols].bitcast(FP8X4), scales=scales[:, cols], in_=grouped[:, first * K : (first + count) * K]
            )

        def mx_pass(acc, operand, i, g, words, plane, start, stop):
            cols = slice((GROUPS * i + g) * P, (GROUPS * i + g + 1) * P)
            nc.tensor.matmul_mx(
                out=acc[:],
                lhsT=operand[1][:, cols].bitcast(FP8X4),
                lhsT_scale=operand[2][:, cols],
                rhs=words.bitcast(FP4X4),
                rhs_scale=plane,
                start=start,
                stop=stop,
            )

        def first_stage(s, i):
            d = ORDER[s][0]
            for h in range(GROUPS):
                z = next_bank([P, BANK])
                for g in range(GROUPS):
                    words = t_words[d, h][:, g, :]
                    plane = plane_of(t_planes, T_RUNS, d, g)[:, h * BANK : (h + 1) * BANK]
                    mx_pass(z, x_ops[s], i, g, words, plane, g == 0, g == GROUPS - 1)
                if h == 0:
                    squares[s, i] = work.tile([P, N], F32, name="squares", bufs=2 * TILES)
                nc.scalar.activation(
                    out=squares[s, i][:, h * BANK : (h + 1) * BANK].rearrange("m (u q e) -> m u q e", u=2, e=2),
                    in_=z[:].rearrange("m (q u e) -> m u q e", u=2, e=2),
                    func=ACT.Square,
                )

        def weigh(s, i, width=N):
            rhos[s, i] = work.tile([P, N], BF16, name="rho", bufs=TILES * (RHO_LAG + 1))
            for c0 in range(0, N, width):
                cols = slice(c0, c0 + width)
                nc.vector.tensor_tensor(
                    out=rhos[s, i][:, cols], in0=squares[s, i][:, cols], in1=gains[ORDER[s][0]][:, cols], op=ALU.mult
                )

        sums, added = {}, {}

        def second_stage(s, i):
            d, half = ORDER[s]
            before = added.get((half, i), 0)
            added[half, i] = before + 1
            if before == 0:
                sums[i] = psum.tile([P, R], F32, name="sum%d" % i)
            for g in range(GROUPS):
                start, stop = before == 0 and g == 0, before == D - 1 and g == GROUPS - 1
                mx_pass(sums[i], rho_ops[s], i, g, c_words[d][:, g, :], plane_of(c_planes, C_RUNS, d, g), start, stop)

        def store(half, i, copy, width=R):
            m0 = (TILES * half + i) * P
            for c0 in range(0, R, width):
                result = work.tile([P, width], F32, name="result%d" % width)
                copy(out=result[:], in_=sums[i][:, c0 : c0 + width])
                nc.sync.dma_start(out=out[m0 : m0 + P, c0 : c0 + width], in_=result[:])

        turn_strain(0, 0)
        turn_gain()
        quantise(x_ops[0], 0, 1)
        warm_up(WARM_BETWEEN)
        for d in range(D - 1):
            spread_gain(d, on_vector if d % 2 == 0 else on_scalar)
        turn_strain(0, 1)
        first_stage(0, 0)
        quantise(x_ops[0], 1, 1)
        spread_gain(D - 1, on_vector)
        weigh(0, 0)

        for s in range(LAST + 1):
            old = s - RHO_LAG
            if old >= 0:
                turn_rho(old, 0, on_scalar)
                turn_rho(old, 1, on_vector)
            if s < LAST:
                for i in range(TILES):
                    turn_strain(s + 1, i)
            if s == LAST:
                for i in range(TILES):
                    store(0, i, on_scalar)
            if FIRST_SORTED <= s + 2 <= LAST:
                sort_strain(s + 2)
            if old >= 0:
                quantise(rho_ops[old])
            if s > 0:
                weigh(s - 1, 1)
            if s < LAST:
                quantise(x_ops[s + 1])
            if s > 0:
                first_stage(s, 0)
                weigh(s, 0)
            first_stage(s, 1)
            if old >= 0 and old != HELD:
                for i in range(TILES):
                    second_stage(old, i)

        weigh(LAST, 1, BANK)
        for i in range(TILES):
            turn_rho(LAST - 1, i, on_scalar)
        turn_rho(LAST, 0, on_scalar)
        quantise(rho_ops[LAST - 1])
        for i in range(TILES):
            second_stage(HELD, i)
        turn_rho(LAST, 1, on_scalar)
        for i in range(TILES):
            quantise(rho_ops[LAST], i, 1)
        for i in range(TILES):
            second_stage(LAST - 1, i)
        second_stage(LAST, 0)
        store(1, 0, on_vector)
        second_stage(LAST, 1)
        store(1, 1, on_scalar, R // 2)
